import numpy as np
import ml_dtypes


def mxq(x, axis, fmt="e4m3"):
    dtype, down = {"e4m3": (ml_dtypes.float8_e4m3fn, 7), "e5m2": (ml_dtypes.float8_e5m2, 14)}[fmt]
    v = np.moveaxis(np.asarray(x, np.float32).astype(ml_dtypes.bfloat16).astype(np.float64), axis, -1)
    blocks = v.reshape(v.shape[:-1] + (-1, 32))
    amax = np.abs(blocks).max(-1, keepdims=True)
    byte = np.maximum(np.where(amax > 0, np.frexp(amax)[1] - 1 + 127, 0) - down, 1)
    scale = np.exp2(byte - 127.0)
    codes = (blocks / scale).astype(np.float32).astype(dtype).astype(np.float64)
    return np.moveaxis((codes * scale).reshape(v.shape), -1, axis)


WIDE = False


def mx_kscale(k):
    if not WIDE:
        return np.ones(k)
    levels = np.array([10, -10, 5, -5, 0])
    if k % 512:
        return np.exp2(np.random.permutation(np.resize(levels, k // 32))).repeat(32)
    a = np.empty((k // 512, 16))
    for p in range(k // 512):
        a[p, :8] = np.random.permutation(np.resize(levels, 8))
        for g in range(8):
            far = levels[np.abs(levels - a[p, g]) >= 10]
            a[p, g + 8] = far[np.random.randint(len(far))]
    return np.exp2(a.ravel()).repeat(32)


def f64(x):
    return np.asarray(x).astype(np.float64)


def striped(idx):
    return np.tile(np.asarray(idx).reshape(-1, 16).T, (8, 1)).astype(np.uint16)


def unstriped(offs):
    return offs[:16].T.reshape(-1).astype(np.int64)


E2M1 = np.array([0.0, 0.5, 1.0, 1.5, 2.0, 3.0, 4.0, 6.0, -0.0, -0.5, -1.0, -1.5, -2.0, -3.0, -4.0, -6.0])


def pack_weight(w, fmt):
    k, n = w.shape
    w = f64(np.asarray(w, np.float32).astype(ml_dtypes.bfloat16)).reshape(k // 32, 32, n)
    amax = np.abs(w).max(1)
    if fmt == "e4m3":
        byte = np.frexp(amax)[1] - 1 + 127 - 7
    else:
        mant, ex = np.frexp(amax / 6.0)
        byte = np.where(mant > 0.5, ex, ex - 1) + 127
    byte = np.clip(np.where(amax > 0, byte, 1), 1, 254)
    scaled = (w * np.exp2(127.0 - byte)[:, None, :]).reshape(k, n).astype(np.float32)
    by_word = np.ascontiguousarray(scaled.reshape(k // 512, 128, 4, n).transpose(0, 1, 3, 2))
    if fmt == "e4m3":
        words = by_word.astype(ml_dtypes.float8_e4m3fn).view(np.uint8)
    else:
        c = by_word.astype(ml_dtypes.float4_e2m1fn).view(np.uint8) & 0xF
        words = (c[..., 0::2] | (c[..., 1::2] << 4)).reshape(k // 512, 128, 2 * n)
    return np.ascontiguousarray(words), np.ascontiguousarray(byte.astype(np.uint8).reshape(k // 512, 16, n))


def unpack_weight(words, scales, fmt):
    g, _, n = scales.shape
    words = np.ascontiguousarray(words).reshape(g, 128, n, -1)
    if fmt == "e4m3":
        vals = words.view(ml_dtypes.float8_e4m3fn).astype(np.float64)
    else:
        nib = np.empty((g, 128, n, 4), np.uint8)
        nib[..., 0::2] = words & 0xF
        nib[..., 1::2] = words >> 4
        vals = E2M1[nib]
    vals = vals * np.repeat(np.exp2(scales.astype(np.float64) - 127.0), 8, axis=1)[..., None]
    return vals.transpose(0, 1, 3, 2).reshape(g * 512, n)


K, T, J, N = 1024, 1024, 512, 512


def setup_inputs():
    n = np.random.standard_normal
    idx = np.random.permutation(T)[:J]
    idx2 = np.random.permutation(T)[:J]
    fk = mx_kscale(K)
    xtp = pack_weight(n((K, T)) / fk[:, None], "e4m3")
    wbp = pack_weight(n((K, N)) * 1 / np.sqrt(K) * fk[:, None], "e2m1")
    return {
        "xt_words": xtp[0],
        "xt_scales": xtp[1],
        "wa": (n((K, N)) * 1 / np.sqrt(K) * fk[:, None]).astype(np.float32),
        "wb_words": wbp[0],
        "wb_scales": wbp[1],
        "ga": (np.random.uniform(0.4, 1.2, (1, J))).astype(np.float32),
        "offs": striped(idx),
        "offs2": striped(idx2),
    }


def reference(xt_words, xt_scales, wa, wb_words, wb_scales, ga, offs, offs2):
    idx = unstriped(offs)
    idx2 = unstriped(offs2)
    xtu = unpack_weight(xt_words, xt_scales, "e4m3")
    wbu = unpack_weight(wb_words, wb_scales, "e2m1")
    waq = mxq(f64(wa), 0, "e4m3")
    xtidxg = xtu[:, idx]
    a = waq.T @ xtidxg
    xtidx2g = xtu[:, idx2]
    b = wbu.T @ xtidx2g
    y = f64(ga) * a * b / (np.abs(a) + np.abs(b) + 0.2)
    return y

@@ -1,0 +1,172 @@
+from contextlib import ExitStack
+
+import concourse.mybir as mybir
+from concourse.masks import make_identity
+
+K, T, J, N = 1024, 1024, 512, 512
+FLOPS = 2 * 2 * K * J * N
+
+F32 = mybir.dt.float32
+BF16 = mybir.dt.bfloat16
+I32 = mybir.dt.int32
+U32 = mybir.dt.uint32
+U16 = mybir.dt.uint16
+U8 = mybir.dt.uint8
+FP8X4 = mybir.dt.float8_e4m3fn_x4
+FP4X4 = mybir.dt.float4_e2m1fn_x4
+ACT = mybir.ActivationFunctionType
+ALU = mybir.AluOpType
+
+P = 128
+PASSES = 2
+HALF = 256
+BLOCKS = N // P
+
+
+def tile_moe_experts_product_over_sizes_kernel(tc, xt_words, xt_scales, wa, wb_words, wb_scales, ga, offs, offs2, out):
+    nc = tc.nc
+    with ExitStack() as ctx:
+        keep = ctx.enter_context(tc.tile_pool(name="keep", bufs=1))
+        psum = ctx.enter_context(tc.psum_pool(name="psum", bufs=1))
+
+        list_a = keep.tile([P, J // 16], U16, name="list_a")
+        list_b = keep.tile([P, J // 16], U16, name="list_b")
+        x_words = [keep.tile([P, T], I32, name="x_words%d" % z, align_bytes=64) for z in range(PASSES)]
+        x_sc_both = keep.tile([P, T], U8, name="x_sc_both", align_bytes=64)
+        x_sc_last = keep.tile([P, T], U8, name="x_sc_last", align_bytes=64)
+        wb_w = keep.tile([P, PASSES, 2 * N], U8, name="wb_w", align_bytes=64)
+        wb_s = keep.tile([P, PASSES, N], U8, name="wb_s", align_bytes=64)
+        ga_col = keep.tile([P, 4], F32, name="ga_col")
+        ident = keep.tile([P, P], F32, name="ident")
+        warm = keep.tile([P, 2], F32, name="warm")
+
+        nc.vector.memset(x_sc_both[:].bitcast(I32), 0)
+        nc.vector.memset(x_sc_last[:].bitcast(I32), 0)
+        nc.vector.memset(wb_s[:].rearrange("p z n -> p (z n)").bitcast(I32), 0)
+        nc.vector.memset(warm[:, 0:1], 1.0)
+        nc.scalar.activation(warm[:, 1:2], warm[:, 0:1], ACT.Abs_reciprocal_sqrt)
+
+        xs32 = xt_scales.bitcast(I32)
+        wbs32 = wb_scales.bitcast(I32).rearrange("z (q r) n -> r q z n", r=4)
+        raw = {}
+
+        def load_wa(z):
+            raw[z] = keep.tile([P, 4, N], F32, name="raw%d" % z)
+            rows = wa[z * 512 : (z + 1) * 512, :]
+            nc.sync.dma_start(raw[z][:], rows.rearrange("(p j) n -> p j n", j=4))
+
+        def load_x(z):
+            nc.sync.dma_start(x_words[z][:], xt_words[z].rearrange("p c r -> p (c r)").bitcast(I32))
+
+        nc.sync.dma_start(list_b[:], offs2)
+        nc.sync.dma_start(list_a[:], offs)
+        load_x(0)
+        for q in range(4):
+            nc.sync.dma_start(x_sc_both[32 * q : 32 * q + 8, :].bitcast(I32), xs32[:, 4 * q : 4 * q + 4, :])
+        load_wa(0)
+        for r in range(4):
+            nc.sync.dma_start(x_sc_last[r:P:32, :].bitcast(I32), xs32[1].rearrange("(q r) n -> r q n", r=4)[r])
+        load_wa(1)
+        load_x(1)
+        for r in range(4):
+            nc.sync.dma_start(wb_s[r:P:32, :, :].bitcast(I32), wbs32[r])
+        nc.sync.dma_start(wb_w[:].bitcast(I32), wb_words.bitcast(I32).rearrange("z p c -> p z c"))
+        nc.gpsimd.dma_start(ga_col[:], ga.rearrange("o (p c) -> (o p) c", c=4))
+        make_identity(nc, ident[:])
+
+        g_ps = psum.tile([P, 4, P], F32, name="g_ps", tag="bank7")
+        for c in range(4):
+            nc.tensor.transpose(g_ps[:, c, :], ga_col[:, c : c + 1].to_broadcast([P, P]), ident[:])
+        g_all = keep.tile([P, P, 4], F32, name="g_all")
+        nc.scalar.copy(g_all[:], g_ps[:].rearrange("m c p -> m p c"))
+        g_row = g_all[:].rearrange("m p c -> m (p c)")
+
+        def gather(name, dtype, window, offsets):
+            picked = keep.tile([P, J], dtype, name=name, align_bytes=64)
+            nc.vector.tensor_copy(picked[:], window.indirect(offsets[:]))
+            return picked
+
+        xb_w0 = gather("xb_w0", U32, x_words[0][:].bitcast(U32), list_b)
+        xa_w0 = gather("xa_w0", U32, x_words[0][:].bitcast(U32), list_a)
+        xb_s0 = gather("xb_s0", U8, x_sc_both[:], list_b)
+        xa_s = gather("xa_s", U8, x_sc_both[:], list_a)
+        xb_s1 = gather("xb_s1", U8, x_sc_last[:], list_b)
+        xb_w1 = gather("xb_w1", U32, x_words[1][:].bitcast(U32), list_b)
+        xa_w1 = gather("xa_w1", U32, x_words[1][:].bitcast(U32), list_a)
+        xb_w, xb_s = [xb_w0, xb_w1], [xb_s0, xb_s1]
+        xa_w = [xa_w0, xa_w1]
+
+        b_ps, b_abs = [], []
+        for nb in range(BLOCKS):
+            b_ps.append(psum.tile([P, J], F32, name="b_ps%d" % nb, tag="bank%d" % nb))
+        for z in range(PASSES):
+            for nb in range(BLOCKS):
+                nc.tensor.matmul_mx(
+                    out=b_ps[nb][:],
+                    lhsT=wb_w[:, z, nb * 2 * P : (nb + 1) * 2 * P].bitcast(FP4X4),
+                    lhsT_scale=wb_s[:, z, nb * P : (nb + 1) * P],
+                    rhs=xb_w[z][:].bitcast(FP8X4),
+                    rhs_scale=xb_s[z][:],
+                    start=(z == 0),
+                    stop=(z == PASSES - 1),
+                )
+
+        wa_w, wa_s = {}, {}
+
+        def quantise(z, h):
+            grouped = keep.tile([P, HALF, 4], BF16, name="grouped%d%d" % (z, h), tag="stage%d%d" % (z, h), align_bytes=64)
+            nc.scalar.copy(
+                grouped[:].rearrange("p (c i) t -> p c t i", i=4),
+                raw[z][:, :, h * HALF : (h + 1) * HALF].rearrange("p t (c i) -> p c t i", i=4),
+            )
+            wa_w[z, h] = keep.tile([P, HALF], U32, name="wa_w%d%d" % (z, h), align_bytes=64)
+            wa_s[z, h] = keep.tile([P, HALF], U8, name="wa_s%d%d" % (z, h), align_bytes=64)
+            nc.vector.quantize_mx(
+                out=wa_w[z, h][:].bitcast(FP8X4),
+                scales=wa_s[z, h][:],
+                in_=grouped[:].rearrange("p n t -> p (n t)"),
+            )
+
+        def b_side(nb):
+            mag = keep.tile([P, J], F32, name="b_abs%d" % nb)
+            nc.scalar.activation(mag[:], b_ps[nb][:], ACT.Abs)
+            nc.vector.tensor_tensor(gated[:, nb, :], b_ps[nb][:], g_row, ALU.mult)
+            b_abs.append(mag)
+
+        def a_side(nb):
+            h, c0 = divmod(nb * P, HALF)
+            bank = psum.tile([P, J], F32, name="a_ps%d" % nb, tag="bank%d" % (4 + nb))
+            for z in range(PASSES):
+                nc.tensor.matmul_mx(
+                    out=bank[:],
+                    lhsT=wa_w[z, h][:, c0 : c0 + P].bitcast(FP8X4),
+                    lhsT_scale=wa_s[z, h][:, c0 : c0 + P],
+                    rhs=xa_w[z][:].bitcast(FP8X4),
+                    rhs_scale=xa_s[4 * z : P, :],
+                    start=(z == 0),
+                    stop=(z == PASSES - 1),
+                )
+            mag = keep.tile([P, J], F32, name="a_abs%d" % nb)
+            nc.scalar.activation(mag[:], bank[:], ACT.Abs)
+            num = keep.tile([P, J], F32, name="num%d" % nb)
+            nc.vector.tensor_tensor(num[:], bank[:], gated[:, nb, :], ALU.mult)
+            total = keep.tile([P, J], F32, name="total%d" % nb)
+            adder = nc.vector if nb == BLOCKS - 1 else nc.gpsimd
+            adder.tensor_tensor(total[:], mag[:], b_abs[nb][:], ALU.add)
+            sq = keep.tile([P, J], F32, name="sq%d" % nb)
+            nc.scalar.activation(sq[:], total[:], ACT.Square, bias=0.2)
+            inv = keep.tile([P, J], F32, name="inv%d" % nb)
+            nc.scalar.activation(inv[:], sq[:], ACT.Abs_reciprocal_sqrt)
+            res = keep.tile([P, J], F32, name="res%d" % nb)
+            nc.vector.tensor_tensor(res[:], num[:], inv[:], ALU.mult)
+            nc.sync.dma_start(out[nb * P : (nb + 1) * P, :], res[:])
+
+        quantise(0, 0)
+        quantise(0, 1)
+        quantise(1, 0)
+        quantise(1, 1)
+        gated = keep.tile([P, BLOCKS, J], F32, name="gated", tag="stage11", align_bytes=64)
+        for nb in range(BLOCKS):
+            b_side(nb)
+        for nb in range(BLOCKS):
+            a_side(nb)

@@ -31,9 +31,9 @@ def tile_moe_experts_product_over_sizes_kernel(tc, xt_words, xt_scales, wa, wb_w
 
         list_a = keep.tile([P, J // 16], U16, name="list_a")
         list_b = keep.tile([P, J // 16], U16, name="list_b")
-        x_words = [keep.tile([P, T], I32, name="x_words%d" % z, align_bytes=64) for z in range(PASSES)]
+        x_words = [keep.tile([P, T], I32, name="x_words%d" % z, tag="x_words%d" % z, align_bytes=64) for z in range(PASSES)]
         x_sc_both = keep.tile([P, T], U8, name="x_sc_both", align_bytes=64)
-        x_sc_last = keep.tile([P, T], U8, name="x_sc_last", align_bytes=64)
+        xb_s1 = keep.tile([P, J], U8, name="xb_s1", align_bytes=64)
         wb_w = keep.tile([P, PASSES, 2 * N], U8, name="wb_w", align_bytes=64)
         wb_s = keep.tile([P, PASSES, N], U8, name="wb_s", align_bytes=64)
         ga_col = keep.tile([P, 4], F32, name="ga_col")
@@ -41,85 +41,83 @@ def tile_moe_experts_product_over_sizes_kernel(tc, xt_words, xt_scales, wa, wb_w
         warm = keep.tile([P, 2], F32, name="warm")
 
         nc.vector.memset(x_sc_both[:].bitcast(I32), 0)
-        nc.vector.memset(x_sc_last[:].bitcast(I32), 0)
-        nc.vector.memset(wb_s[:].rearrange("p z n -> p (z n)").bitcast(I32), 0)
+        nc.vector.memset(xb_s1[:].bitcast(I32), 0)
+        nc.gpsimd.memset(wb_s[:].rearrange("p z n -> p (z n)").bitcast(I32), 0)
         nc.vector.memset(warm[:, 0:1], 1.0)
         nc.scalar.activation(warm[:, 1:2], warm[:, 0:1], ACT.Abs_reciprocal_sqrt)
 
         xs32 = xt_scales.bitcast(I32)
-        wbs32 = wb_scales.bitcast(I32).rearrange("z (q r) n -> r q z n", r=4)
+        wbs32 = wb_scales.bitcast(I32).rearrange("z (q r) n -> q r z n", r=4)
         raw = {}
 
-        def load_wa(z):
-            raw[z] = keep.tile([P, 4, N], F32, name="raw%d" % z)
-            rows = wa[z * 512 : (z + 1) * 512, :]
-            nc.sync.dma_start(raw[z][:], rows.rearrange("(p j) n -> p j n", j=4))
+        def load_wa(z, n0, n1, slot):
+            tile = keep.tile([P, 4, n1 - n0], F32, name="raw%d_%d" % (z, n0), tag=slot)
+            rows = wa[z * 512 : (z + 1) * 512, n0:n1]
+            nc.sync.dma_start(tile[:], rows.rearrange("(p j) n -> p j n", j=4))
+            for h in range(n0 // HALF, n1 // HALF):
+                raw[z, h] = tile[:, :, h * HALF - n0 : (h + 1) * HALF - n0]
 
         def load_x(z):
             nc.sync.dma_start(x_words[z][:], xt_words[z].rearrange("p c r -> p (c r)").bitcast(I32))
 
+        def gather(name, dtype, window, offsets, slot=None):
+            picked = keep.tile([P, J], dtype, name=name, tag=slot or name, align_bytes=64)
+            nc.vector.tensor_copy(picked[:], window.indirect(offsets[:]))
+            return picked
+
         nc.sync.dma_start(list_b[:], offs2)
-        nc.sync.dma_start(list_a[:], offs)
-        load_x(0)
         for q in range(4):
             nc.sync.dma_start(x_sc_both[32 * q : 32 * q + 8, :].bitcast(I32), xs32[:, 4 * q : 4 * q + 4, :])
-        load_wa(0)
-        for r in range(4):
-            nc.sync.dma_start(x_sc_last[r:P:32, :].bitcast(I32), xs32[1].rearrange("(q r) n -> r q n", r=4)[r])
-        load_wa(1)
-        load_x(1)
-        for r in range(4):
-            nc.sync.dma_start(wb_s[r:P:32, :, :].bitcast(I32), wbs32[r])
+        nc.sync.dma_start(list_a[:], offs)
+        load_x(0)
         nc.sync.dma_start(wb_w[:].bitcast(I32), wb_words.bitcast(I32).rearrange("z p c -> p z c"))
+        for q in range(4):
+            nc.sync.dma_start(wb_s[32 * q : 32 * q + 4, :, :].bitcast(I32), wbs32[q])
+        load_wa(0, 0, HALF, "raw_first")
+        load_wa(0, HALF, N, "raw_second")
+        load_x(1)
+        load_wa(1, 0, HALF, "raw_third")
+        xb_s0 = gather("xb_s0", U8, x_sc_both[:], list_b)
+        for q in range(4):
+            nc.sync.dma_start(xb_s1[32 * q : 32 * q + 4, :].bitcast(I32), xb_s0[32 * q + 4 : 32 * q + 8, :].bitcast(I32))
+        load_wa(1, HALF, N, "raw_fourth")
         nc.gpsimd.dma_start(ga_col[:], ga.rearrange("o (p c) -> (o p) c", c=4))
         make_identity(nc, ident[:])
 
         g_ps = psum.tile([P, 4, P], F32, name="g_ps", tag="bank7")
         for c in range(4):
             nc.tensor.transpose(g_ps[:, c, :], ga_col[:, c : c + 1].to_broadcast([P, P]), ident[:])
-        g_all = keep.tile([P, P, 4], F32, name="g_all")
-        nc.scalar.copy(g_all[:], g_ps[:].rearrange("m c p -> m p c"))
-        g_row = g_all[:].rearrange("m p c -> m (p c)")
 
-        def gather(name, dtype, window, offsets):
-            picked = keep.tile([P, J], dtype, name=name, align_bytes=64)
-            nc.vector.tensor_copy(picked[:], window.indirect(offsets[:]))
-            return picked
-
+        xa_s = gather("xa_s", U8, x_sc_both[:], list_a)
         xb_w0 = gather("xb_w0", U32, x_words[0][:].bitcast(U32), list_b)
         xa_w0 = gather("xa_w0", U32, x_words[0][:].bitcast(U32), list_a)
-        xb_s0 = gather("xb_s0", U8, x_sc_both[:], list_b)
-        xa_s = gather("xa_s", U8, x_sc_both[:], list_a)
-        xb_s1 = gather("xb_s1", U8, x_sc_last[:], list_b)
-        xb_w1 = gather("xb_w1", U32, x_words[1][:].bitcast(U32), list_b)
-        xa_w1 = gather("xa_w1", U32, x_words[1][:].bitcast(U32), list_a)
-        xb_w, xb_s = [xb_w0, xb_w1], [xb_s0, xb_s1]
-        xa_w = [xa_w0, xa_w1]
 
-        b_ps, b_abs = [], []
-        for nb in range(BLOCKS):
-            b_ps.append(psum.tile([P, J], F32, name="b_ps%d" % nb, tag="bank%d" % nb))
-        for z in range(PASSES):
+        b_ps = [psum.tile([P, J], F32, name="b_ps%d" % nb, tag="bank%d" % nb) for nb in range(BLOCKS)]
+        a_ps = [psum.tile([P, J], F32, name="a_ps%d" % nb, tag="bank%d" % (4 + nb)) for nb in range(BLOCKS)]
+
+        def b_pass(z, words, scales):
             for nb in range(BLOCKS):
                 nc.tensor.matmul_mx(
                     out=b_ps[nb][:],
                     lhsT=wb_w[:, z, nb * 2 * P : (nb + 1) * 2 * P].bitcast(FP4X4),
                     lhsT_scale=wb_s[:, z, nb * P : (nb + 1) * P],
-                    rhs=xb_w[z][:].bitcast(FP8X4),
-                    rhs_scale=xb_s[z][:],
+                    rhs=words[:].bitcast(FP8X4),
+                    rhs_scale=scales[:],
                     start=(z == 0),
                     stop=(z == PASSES - 1),
                 )
 
+        b_pass(0, xb_w0, xb_s0)
+
         wa_w, wa_s = {}, {}
 
-        def quantise(z, h):
+        def quantise(z, h, copy, slot=None):
             grouped = keep.tile([P, HALF, 4], BF16, name="grouped%d%d" % (z, h), tag="stage%d%d" % (z, h), align_bytes=64)
-            nc.scalar.copy(
+            copy(
                 grouped[:].rearrange("p (c i) t -> p c t i", i=4),
-                raw[z][:, :, h * HALF : (h + 1) * HALF].rearrange("p t (c i) -> p c t i", i=4),
+                raw[z, h].rearrange("p t (c i) -> p c t i", i=4),
             )
-            wa_w[z, h] = keep.tile([P, HALF], U32, name="wa_w%d%d" % (z, h), align_bytes=64)
+            wa_w[z, h] = keep.tile([P, HALF], U32, name="wa_w%d%d" % (z, h), tag=slot or "wa_w%d%d" % (z, h), align_bytes=64)
             wa_s[z, h] = keep.tile([P, HALF], U8, name="wa_s%d%d" % (z, h), align_bytes=64)
             nc.vector.quantize_mx(
                 out=wa_w[z, h][:].bitcast(FP8X4),
@@ -127,18 +125,23 @@ def tile_moe_experts_product_over_sizes_kernel(tc, xt_words, xt_scales, wa, wb_w
                 in_=grouped[:].rearrange("p n t -> p (n t)"),
             )
 
-        def b_side(nb):
-            mag = keep.tile([P, J], F32, name="b_abs%d" % nb)
-            nc.scalar.activation(mag[:], b_ps[nb][:], ACT.Abs)
-            nc.vector.tensor_tensor(gated[:, nb, :], b_ps[nb][:], g_row, ALU.mult)
-            b_abs.append(mag)
+        quantise(0, 0, nc.scalar.copy)
+        quantise(0, 1, nc.scalar.copy)
+        g_all = keep.tile([P, P, 4], F32, name="g_all", tag="raw_second")
+        nc.scalar.copy(g_all[:], g_ps[:].rearrange("m c p -> m p c"))
+        g_row = g_all[:].rearrange("m p c -> m (p c)")
 
-        def a_side(nb):
-            h, c0 = divmod(nb * P, HALF)
-            bank = psum.tile([P, J], F32, name="a_ps%d" % nb, tag="bank%d" % (4 + nb))
-            for z in range(PASSES):
+        xb_w1 = gather("xb_w1", U32, x_words[1][:].bitcast(U32), list_b, "stage01")
+        xa_w1 = gather("xa_w1", U32, x_words[1][:].bitcast(U32), list_a, "xb_s0")
+        quantise(1, 0, nc.scalar.copy, "x_words1")
+        xa_w = [xa_w0, xa_w1]
+        quantise(1, 1, nc.vector.tensor_copy)
+
+        def a_pass(z, blocks):
+            for nb in blocks:
+                h, c0 = divmod(nb * P, HALF)
                 nc.tensor.matmul_mx(
-                    out=bank[:],
+                    out=a_ps[nb][:],
                     lhsT=wa_w[z, h][:, c0 : c0 + P].bitcast(FP8X4),
                     lhsT_scale=wa_s[z, h][:, c0 : c0 + P],
                     rhs=xa_w[z][:].bitcast(FP8X4),
@@ -146,27 +149,42 @@ def tile_moe_experts_product_over_sizes_kernel(tc, xt_words, xt_scales, wa, wb_w
                     start=(z == 0),
                     stop=(z == PASSES - 1),
                 )
-            mag = keep.tile([P, J], F32, name="a_abs%d" % nb)
-            nc.scalar.activation(mag[:], bank[:], ACT.Abs)
-            num = keep.tile([P, J], F32, name="num%d" % nb)
-            nc.vector.tensor_tensor(num[:], bank[:], gated[:, nb, :], ALU.mult)
-            total = keep.tile([P, J], F32, name="total%d" % nb)
-            adder = nc.vector if nb == BLOCKS - 1 else nc.gpsimd
-            adder.tensor_tensor(total[:], mag[:], b_abs[nb][:], ALU.add)
-            sq = keep.tile([P, J], F32, name="sq%d" % nb)
-            nc.scalar.activation(sq[:], total[:], ACT.Square, bias=0.2)
-            inv = keep.tile([P, J], F32, name="inv%d" % nb)
-            nc.scalar.activation(inv[:], sq[:], ACT.Abs_reciprocal_sqrt)
-            res = keep.tile([P, J], F32, name="res%d" % nb)
-            nc.vector.tensor_tensor(res[:], num[:], inv[:], ALU.mult)
-            nc.sync.dma_start(out[nb * P : (nb + 1) * P, :], res[:])
 
-        quantise(0, 0)
-        quantise(0, 1)
-        quantise(1, 0)
-        quantise(1, 1)
+        a_pass(0, range(BLOCKS))
+        b_pass(1, xb_w1, xb_s1)
+        a_pass(1, range(BLOCKS))
+
+        b_abs = keep.tile([P, BLOCKS, J], F32, name="b_abs", tag="raw_third")
         gated = keep.tile([P, BLOCKS, J], F32, name="gated", tag="stage11", align_bytes=64)
         for nb in range(BLOCKS):
-            b_side(nb)
+            nc.scalar.activation(b_abs[:, nb, :], b_ps[nb][:], ACT.Abs)
+            nc.vector.tensor_tensor(gated[:, nb, :], b_ps[nb][:], g_row, ALU.mult)
+
+        def fresh(name):
+            return [keep.tile([P, J], F32, name="%s%d" % (name, nb)) for nb in range(BLOCKS)]
+
+        a_abs, num, total, sq, inv, res = [fresh(name) for name in ("a_abs", "num", "total", "sq", "inv", "res")]
+
         for nb in range(BLOCKS):
-            a_side(nb)
+            nc.scalar.activation(a_abs[nb][:], a_ps[nb][:], ACT.Abs)
+            adder = nc.vector if nb == 1 else nc.gpsimd
+            adder.tensor_tensor(total[nb][:], a_abs[nb][:], b_abs[:, nb, :], ALU.add)
+        for nb in range(BLOCKS):
+            nc.vector.tensor_tensor(num[nb][:], a_ps[nb][:], gated[:, nb, :], ALU.mult)
+
+        def square(nb):
+            nc.scalar.activation(sq[nb][:], total[nb][:], ACT.Square, bias=0.2)
+
+        def finish(nb):
+            width = J // 2 if nb == BLOCKS - 1 else J
+            for j0 in range(0, J, width):
+                cols = slice(j0, j0 + width)
+                nc.scalar.activation(inv[nb][:, cols], sq[nb][:, cols], ACT.Abs_reciprocal_sqrt)
+                nc.vector.tensor_tensor(res[nb][:, cols], num[nb][:, cols], inv[nb][:, cols], ALU.mult)
+                nc.sync.dma_start(out[nb * P : (nb + 1) * P, cols], res[nb][:, cols])
+
+        square(0)
+        for nb in range(BLOCKS):
+            if nb + 1 < BLOCKS:
+                square(nb + 1)
+            finish(nb)

@@ -73,13 +73,12 @@ def tile_moe_experts_product_over_sizes_kernel(tc, xt_words, xt_scales, wa, wb_w
         nc.sync.dma_start(wb_w[:].bitcast(I32), wb_words.bitcast(I32).rearrange("z p c -> p z c"))
         for q in range(4):
             nc.sync.dma_start(wb_s[32 * q : 32 * q + 4, :, :].bitcast(I32), wbs32[q])
-        load_wa(0, 0, HALF, "raw_first")
-        load_wa(0, HALF, N, "raw_second")
-        load_x(1)
-        load_wa(1, 0, HALF, "raw_third")
+        load_wa(0, 0, N, "raw_first")
         xb_s0 = gather("xb_s0", U8, x_sc_both[:], list_b)
         for q in range(4):
             nc.sync.dma_start(xb_s1[32 * q : 32 * q + 4, :].bitcast(I32), xb_s0[32 * q + 4 : 32 * q + 8, :].bitcast(I32))
+        load_x(1)
+        load_wa(1, 0, HALF, "raw_third")
         load_wa(1, HALF, N, "raw_fourth")
         nc.gpsimd.dma_start(ga_col[:], ga.rearrange("o (p c) -> (o p) c", c=4))
         make_identity(nc, ident[:])
@@ -111,29 +110,30 @@ def tile_moe_experts_product_over_sizes_kernel(tc, xt_words, xt_scales, wa, wb_w
 
         wa_w, wa_s = {}, {}
 
-        def quantise(z, h, copy, slot=None):
-            grouped = keep.tile([P, HALF, 4], BF16, name="grouped%d%d" % (z, h), tag="stage%d%d" % (z, h), align_bytes=64)
+        def quantise(z, h, copy):
+            grouped = keep.tile([P, HALF, 4], BF16, name="grouped%d%d" % (z, h), tag="stage%d%d" % (z, h * (1 - z)), align_bytes=64)
             copy(
                 grouped[:].rearrange("p (c i) t -> p c t i", i=4),
                 raw[z, h].rearrange("p t (c i) -> p c t i", i=4),
             )
-            wa_w[z, h] = keep.tile([P, HALF], U32, name="wa_w%d%d" % (z, h), tag=slot or "wa_w%d%d" % (z, h), align_bytes=64)
+            wa_w[z, h] = codes[:, z, h * HALF : (h + 1) * HALF]
             wa_s[z, h] = keep.tile([P, HALF], U8, name="wa_s%d%d" % (z, h), align_bytes=64)
             nc.vector.quantize_mx(
-                out=wa_w[z, h][:].bitcast(FP8X4),
+                out=wa_w[z, h].bitcast(FP8X4),
                 scales=wa_s[z, h][:],
                 in_=grouped[:].rearrange("p n t -> p (n t)"),
             )
 
-        quantise(0, 0, nc.scalar.copy)
-        quantise(0, 1, nc.scalar.copy)
-        g_all = keep.tile([P, P, 4], F32, name="g_all", tag="raw_second")
+        g_all = keep.tile([P, P, 4], F32, name="g_all")
         nc.scalar.copy(g_all[:], g_ps[:].rearrange("m c p -> m p c"))
         g_row = g_all[:].rearrange("m p c -> m (p c)")
 
-        xb_w1 = gather("xb_w1", U32, x_words[1][:].bitcast(U32), list_b, "stage01")
-        xa_w1 = gather("xa_w1", U32, x_words[1][:].bitcast(U32), list_a, "xb_s0")
-        quantise(1, 0, nc.scalar.copy, "x_words1")
+        xb_w1 = gather("xb_w1", U32, x_words[1][:].bitcast(U32), list_b)
+        xa_w1 = gather("xa_w1", U32, x_words[1][:].bitcast(U32), list_a)
+        codes = keep.tile([P, PASSES, N], U32, name="codes", tag="x_words1", align_bytes=64)
+        quantise(0, 0, nc.scalar.copy)
+        quantise(0, 1, nc.scalar.copy)
+        quantise(1, 0, nc.scalar.copy)
         xa_w = [xa_w0, xa_w1]
         quantise(1, 1, nc.vector.tensor_copy)
 
@@ -155,7 +155,7 @@ def tile_moe_experts_product_over_sizes_kernel(tc, xt_words, xt_scales, wa, wb_w
         a_pass(1, range(BLOCKS))
 
         b_abs = keep.tile([P, BLOCKS, J], F32, name="b_abs", tag="raw_third")
-        gated = keep.tile([P, BLOCKS, J], F32, name="gated", tag="stage11", align_bytes=64)
+        gated = keep.tile([P, BLOCKS, J], F32, name="gated", tag="stage10", align_bytes=64)
         for nb in range(BLOCKS):
             nc.scalar.activation(b_abs[:, nb, :], b_ps[nb][:], ACT.Abs)
             nc.vector.tensor_tensor(gated[:, nb, :], b_ps[nb][:], g_row, ALU.mult)

from contextlib import ExitStack

import concourse.mybir as mybir
from concourse.masks import make_identity

K, T, J, N = 1024, 1024, 512, 512
FLOPS = 2 * 2 * K * J * N

F32 = mybir.dt.float32
BF16 = mybir.dt.bfloat16
I32 = mybir.dt.int32
U32 = mybir.dt.uint32
U16 = mybir.dt.uint16
U8 = mybir.dt.uint8
FP8X4 = mybir.dt.float8_e4m3fn_x4
FP4X4 = mybir.dt.float4_e2m1fn_x4
ACT = mybir.ActivationFunctionType
ALU = mybir.AluOpType

P = 128
PASSES = 2
HALF = 256
BLOCKS = N // P


def tile_moe_experts_product_over_sizes_kernel(tc, xt_words, xt_scales, wa, wb_words, wb_scales, ga, offs, offs2, out):
    nc = tc.nc
    with ExitStack() as ctx:
        keep = ctx.enter_context(tc.tile_pool(name="keep", bufs=1))
        psum = ctx.enter_context(tc.psum_pool(name="psum", bufs=1))

        list_a = keep.tile([P, J // 16], U16, name="list_a")
        list_b = keep.tile([P, J // 16], U16, name="list_b")
        x_words = [keep.tile([P, T], I32, name="x_words%d" % z, tag="x_words%d" % z, align_bytes=64) for z in range(PASSES)]
        x_sc_both = keep.tile([P, T], U8, name="x_sc_both", align_bytes=64)
        xb_s1 = keep.tile([P, J], U8, name="xb_s1", align_bytes=64)
        wb_w = keep.tile([P, PASSES, 2 * N], U8, name="wb_w", align_bytes=64)
        wb_s = keep.tile([P, PASSES, N], U8, name="wb_s", align_bytes=64)
        ga_col = keep.tile([P, 4], F32, name="ga_col")
        ident = keep.tile([P, P], F32, name="ident")
        warm = keep.tile([P, 2], F32, name="warm")

        nc.vector.memset(x_sc_both[:].bitcast(I32), 0)
        nc.vector.memset(xb_s1[:].bitcast(I32), 0)
        nc.gpsimd.memset(wb_s[:].rearrange("p z n -> p (z n)").bitcast(I32), 0)
        nc.vector.memset(warm[:, 0:1], 1.0)
        nc.scalar.activation(warm[:, 1:2], warm[:, 0:1], ACT.Abs_reciprocal_sqrt)

        xs32 = xt_scales.bitcast(I32)
        wbs32 = wb_scales.bitcast(I32).rearrange("z (q r) n -> q r z n", r=4)
        raw = {}

        def load_wa(z, n0, n1, slot):
            tile = keep.tile([P, 4, n1 - n0], F32, name="raw%d_%d" % (z, n0), tag=slot)
            rows = wa[z * 512 : (z + 1) * 512, n0:n1]
            nc.sync.dma_start(tile[:], rows.rearrange("(p j) n -> p j n", j=4))
            for h in range(n0 // HALF, n1 // HALF):
                raw[z, h] = tile[:, :, h * HALF - n0 : (h + 1) * HALF - n0]

        def load_x(z):
            nc.sync.dma_start(x_words[z][:], xt_words[z].rearrange("p c r -> p (c r)").bitcast(I32))

        def gather(name, dtype, window, offsets, slot=None):
            picked = keep.tile([P, J], dtype, name=name, tag=slot or name, align_bytes=64)
            nc.vector.tensor_copy(picked[:], window.indirect(offsets[:]))
            return picked

        nc.sync.dma_start(list_b[:], offs2)
        for q in range(4):
            nc.sync.dma_start(x_sc_both[32 * q : 32 * q + 8, :].bitcast(I32), xs32[:, 4 * q : 4 * q + 4, :])
        nc.sync.dma_start(list_a[:], offs)
        load_x(0)
        nc.sync.dma_start(wb_w[:].bitcast(I32), wb_words.bitcast(I32).rearrange("z p c -> p z c"))
        for q in range(4):
            nc.sync.dma_start(wb_s[32 * q : 32 * q + 4, :, :].bitcast(I32), wbs32[q])
        load_wa(0, 0, N, "raw_first")
        xb_s0 = gather("xb_s0", U8, x_sc_both[:], list_b)
        for q in range(4):
            nc.sync.dma_start(xb_s1[32 * q : 32 * q + 4, :].bitcast(I32), xb_s0[32 * q + 4 : 32 * q + 8, :].bitcast(I32))
        load_x(1)
        load_wa(1, 0, HALF, "raw_third")
        load_wa(1, HALF, N, "raw_fourth")
        nc.gpsimd.dma_start(ga_col[:], ga.rearrange("o (p c) -> (o p) c", c=4))
        make_identity(nc, ident[:])

        g_ps = psum.tile([P, 4, P], F32, name="g_ps", tag="bank7")
        for c in range(4):
            nc.tensor.transpose(g_ps[:, c, :], ga_col[:, c : c + 1].to_broadcast([P, P]), ident[:])

        xa_s = gather("xa_s", U8, x_sc_both[:], list_a)
        xb_w0 = gather("xb_w0", U32, x_words[0][:].bitcast(U32), list_b)
        xa_w0 = gather("xa_w0", U32, x_words[0][:].bitcast(U32), list_a)

        b_ps = [psum.tile([P, J], F32, name="b_ps%d" % nb, tag="bank%d" % nb) for nb in range(BLOCKS)]
        a_ps = [psum.tile([P, J], F32, name="a_ps%d" % nb, tag="bank%d" % (4 + nb)) for nb in range(BLOCKS)]

        def b_pass(z, words, scales):
            for nb in range(BLOCKS):
                nc.tensor.matmul_mx(
                    out=b_ps[nb][:],
                    lhsT=wb_w[:, z, nb * 2 * P : (nb + 1) * 2 * P].bitcast(FP4X4),
                    lhsT_scale=wb_s[:, z, nb * P : (nb + 1) * P],
                    rhs=words[:].bitcast(FP8X4),
                    rhs_scale=scales[:],
                    start=(z == 0),
                    stop=(z == PASSES - 1),
                )

        b_pass(0, xb_w0, xb_s0)

        wa_w, wa_s = {}, {}

        def quantise(z, h, copy):
            grouped = keep.tile([P, HALF, 4], BF16, name="grouped%d%d" % (z, h), tag="stage%d%d" % (z, h * (1 - z)), align_bytes=64)
            copy(
                grouped[:].rearrange("p (c i) t -> p c t i", i=4),
                raw[z, h].rearrange("p t (c i) -> p c t i", i=4),
            )
            wa_w[z, h] = codes[:, z, h * HALF : (h + 1) * HALF]
            wa_s[z, h] = keep.tile([P, HALF], U8, name="wa_s%d%d" % (z, h), align_bytes=64)
            nc.vector.quantize_mx(
                out=wa_w[z, h].bitcast(FP8X4),
                scales=wa_s[z, h][:],
                in_=grouped[:].rearrange("p n t -> p (n t)"),
            )

        g_all = keep.tile([P, P, 4], F32, name="g_all")
        nc.scalar.copy(g_all[:], g_ps[:].rearrange("m c p -> m p c"))
        g_row = g_all[:].rearrange("m p c -> m (p c)")

        xb_w1 = gather("xb_w1", U32, x_words[1][:].bitcast(U32), list_b)
        xa_w1 = gather("xa_w1", U32, x_words[1][:].bitcast(U32), list_a)
        codes = keep.tile([P, PASSES, N], U32, name="codes", tag="x_words1", align_bytes=64)
        quantise(0, 0, nc.scalar.copy)
        quantise(0, 1, nc.scalar.copy)
        quantise(1, 0, nc.scalar.copy)
        xa_w = [xa_w0, xa_w1]
        quantise(1, 1, nc.vector.tensor_copy)

        def a_pass(z, blocks):
            for nb in blocks:
                h, c0 = divmod(nb * P, HALF)
                nc.tensor.matmul_mx(
                    out=a_ps[nb][:],
                    lhsT=wa_w[z, h][:, c0 : c0 + P].bitcast(FP8X4),
                    lhsT_scale=wa_s[z, h][:, c0 : c0 + P],
                    rhs=xa_w[z][:].bitcast(FP8X4),
                    rhs_scale=xa_s[4 * z : P, :],
                    start=(z == 0),
                    stop=(z == PASSES - 1),
                )

        a_pass(0, range(BLOCKS))
        b_pass(1, xb_w1, xb_s1)
        a_pass(1, range(BLOCKS))

        b_abs = keep.tile([P, BLOCKS, J], F32, name="b_abs", tag="raw_third")
        gated = keep.tile([P, BLOCKS, J], F32, name="gated", tag="stage10", align_bytes=64)
        for nb in range(BLOCKS):
            nc.scalar.activation(b_abs[:, nb, :], b_ps[nb][:], ACT.Abs)
            nc.vector.tensor_tensor(gated[:, nb, :], b_ps[nb][:], g_row, ALU.mult)

        def fresh(name):
            return [keep.tile([P, J], F32, name="%s%d" % (name, nb)) for nb in range(BLOCKS)]

        a_abs, num, total, sq, inv, res = [fresh(name) for name in ("a_abs", "num", "total", "sq", "inv", "res")]

        for nb in range(BLOCKS):
            nc.scalar.activation(a_abs[nb][:], a_ps[nb][:], ACT.Abs)
            adder = nc.vector if nb == 1 else nc.gpsimd
            adder.tensor_tensor(total[nb][:], a_abs[nb][:], b_abs[:, nb, :], ALU.add)
        for nb in range(BLOCKS):
            nc.vector.tensor_tensor(num[nb][:], a_ps[nb][:], gated[:, nb, :], ALU.mult)

        def square(nb):
            nc.scalar.activation(sq[nb][:], total[nb][:], ACT.Square, bias=0.2)

        def finish(nb):
            width = J // 2 if nb == BLOCKS - 1 else J
            for j0 in range(0, J, width):
                cols = slice(j0, j0 + width)
                nc.scalar.activation(inv[nb][:, cols], sq[nb][:, cols], ACT.Abs_reciprocal_sqrt)
                nc.vector.tensor_tensor(res[nb][:, cols], num[nb][:, cols], inv[nb][:, cols], ALU.mult)
                nc.sync.dma_start(out[nb * P : (nb + 1) * P, cols], res[nb][:, cols])

        square(0)
        for nb in range(BLOCKS):
            if nb + 1 < BLOCKS:
                square(nb + 1)
            finish(nb)
